import numpy as np
import ml_dtypes


def mxq(x, axis, fmt="e4m3"):
    dtype, down = {"e4m3": (ml_dtypes.float8_e4m3fn, 7), "e5m2": (ml_dtypes.float8_e5m2, 14)}[fmt]
    v = np.moveaxis(np.asarray(x, np.float32).astype(ml_dtypes.bfloat16).astype(np.float64), axis, -1)
    blocks = v.reshape(v.shape[:-1] + (-1, 32))
    amax = np.abs(blocks).max(-1, keepdims=True)
    byte = np.maximum(np.where(amax > 0, np.frexp(amax)[1] - 1 + 127, 0) - down, 1)
    scale = np.exp2(byte - 127.0)
    codes = (blocks / scale).astype(np.float32).astype(dtype).astype(np.float64)
    return np.moveaxis((codes * scale).reshape(v.shape), -1, axis)


WIDE = False


def mx_kscale(k):
    if not WIDE:
        return np.ones(k)
    levels = np.array([10, -10, 5, -5, 0])
    if k % 512:
        return np.exp2(np.random.permutation(np.resize(levels, k // 32))).repeat(32)
    a = np.empty((k // 512, 16))
    for p in range(k // 512):
        a[p, :8] = np.random.permutation(np.resize(levels, 8))
        for g in range(8):
            far = levels[np.abs(levels - a[p, g]) >= 10]
            a[p, g + 8] = far[np.random.randint(len(far))]
    return np.exp2(a.ravel()).repeat(32)


def f64(x):
    return np.asarray(x).astype(np.float64)


def striped(idx):
    return np.tile(idx.reshape(-1, 16).T, (8, 1)).astype(np.uint16)


def unstriped(offs):
    return offs[:16].T.reshape(-1).astype(np.int64)


def pack_weight(w):
    k, n = w.shape
    w = f64(np.asarray(w, np.float32).astype(ml_dtypes.bfloat16)).reshape(k // 32, 32, n)
    amax = np.abs(w).max(1)
    byte = np.clip(np.where(amax > 0, np.frexp(amax)[1] - 1 + 127 - 7, 1), 1, 254)
    scaled = (w * np.exp2(127.0 - byte)[:, None, :]).reshape(k, n).astype(np.float32)
    words = np.ascontiguousarray(scaled.reshape(k // 512, 128, 4, n).transpose(0, 1, 3, 2)).astype(ml_dtypes.float8_e4m3fn).view(np.uint8)
    return words, np.ascontiguousarray(byte.astype(np.uint8).reshape(k // 512, 16, n))


def unpack_weight(words, scales):
    g, p, n, _ = words.shape
    vals = np.ascontiguousarray(words).view(ml_dtypes.float8_e4m3fn).astype(np.float64) * np.repeat(np.exp2(scales.astype(np.float64) - 127.0), 8, axis=1)[..., None]
    return vals.transpose(0, 1, 3, 2).reshape(g * 512, n)


def relu2(v):
    return np.maximum(v, 0.0) ** 2


K, T, E, C, N = 2048, 768, 12, 128, 128
TOP = 3
PAD = 64


def by_expert(wq, xq):
    return np.concatenate([wq[e].T @ xq[:, e * C:(e + 1) * C] for e in range(E)], axis=1)


def setup_inputs():
    n = np.random.standard_normal
    s = mx_kscale(K)[:, None]
    slot_token = np.empty(E * C, np.int64); pos = np.tile(E * C + np.arange(T) % PAD, (TOP, 1)); taken = np.zeros(T, np.int64)
    liked = np.random.randn(T)
    for e in np.random.permutation(E):
        free = np.flatnonzero(taken < TOP); pick = np.random.permutation(free[np.argsort(-(liked[free] + np.random.gumbel(size=free.size)))[:C]]); slot_token[e * C:(e + 1) * C] = pick
        pos[taken[pick], pick] = e * C + np.arange(C); taken[pick] += 1
    g = np.random.uniform(0.2, 0.8, (TOP, T))
    packed = [pack_weight(m) for m in n((E, K, N)) / np.sqrt(K) / s[None]]
    return {
        "xT": (n((K, T)) * s).astype(np.float32),
        "w_words": np.stack([m[0] for m in packed]),
        "w_scales": np.stack([m[1] for m in packed]),
        "b": (0.3 * n((N, E))).astype(np.float32),
        "gate": np.stack([np.tile(r, (N, 1)) for r in g]).astype(np.float32),
        "offs": striped(slot_token),
        "pos1": striped(pos[0]),
        "pos2": striped(pos[1]),
        "pos3": striped(pos[2]),
    }


def reference(xT, w_words, w_scales, b, gate, offs, pos1, pos2, pos3):
    idx = unstriped(offs)
    w = np.stack([unpack_weight(w_words[e], w_scales[e]) for e in range(E)])
    xq = mxq(f64(xT)[:, idx], 0, "e4m3")
    y = by_expert(w, xq)
    y = relu2(y + np.repeat(f64(b), C, axis=1))
    y = np.concatenate([y, np.zeros((N, PAD))], axis=1)
    return sum(f64(gate[r]) * y[:, unstriped(p)] for r, p in enumerate((pos1, pos2, pos3)))

@@ -1,0 +1,147 @@
+from contextlib import ExitStack
+
+import concourse.mybir as mybir
+
+K, T, E, C, N = 2048, 768, 12, 128, 128
+PAD = 64
+SLOTS = E * C
+FLOPS = 2 * SLOTS * K * N
+
+F32 = mybir.dt.float32
+BF16 = mybir.dt.bfloat16
+I32 = mybir.dt.int32
+U32 = mybir.dt.uint32
+U16 = mybir.dt.uint16
+U8 = mybir.dt.uint8
+FP8X4 = mybir.dt.float8_e4m3fn_x4
+ACT = mybir.ActivationFunctionType
+ALU = mybir.AluOpType
+
+P = 128
+PACK = 4
+PASSES = K // (P * PACK)
+LANES = 16
+
+CHUNKS = [
+    [(256, "v"), (256, "v"), (128, "s"), (128, "v")],
+    [(256, "s"), (256, "s"), (256, "s")],
+    [(256, "s"), (256, "s"), (256, "s")],
+    [(256, "s"), (256, "s"), (256, "s")],
+]
+BYTE_PIECES = [(0, 4), (4, 8), (8, 12)]
+WORD_PIECES = [[(0, 4)], [(4, 8)], [(8, 11), (11, 12)]]
+W_LOADS = [(0, 4), (4, 8), (8, 12)]
+OUT_CHUNKS = [(0, 512), (512, 768)]
+
+
+def tile_moe_ecr_lin_relu2_kernel(tc, xT, w_words, w_scales, b, gate, offs, pos1, pos2, pos3, out):
+    nc = tc.nc
+    with ExitStack() as ctx:
+        keep = ctx.enter_context(tc.tile_pool(name="keep", bufs=1))
+        psum = ctx.enter_context(tc.psum_pool(name="psum", bufs=8))
+
+        offs_sb = keep.tile([P, SLOTS // LANES], U16, name="offs_sb")
+        pos_sb = [keep.tile([P, T // LANES], U16, name="pos_sb%d" % r) for r in range(3)]
+        bias = keep.tile([P, E], F32, name="bias")
+        w_codes = keep.tile([P, E * PASSES, N], I32, name="w_codes", align_bytes=64)
+        w_plane = keep.tile([P, E * PASSES, N], U8, name="w_plane", align_bytes=64)
+        gates = [keep.tile([P, T], F32, name="gates%d" % r) for r in range(3)]
+        tok_codes = [keep.tile([P, T], U32, name="tok_codes%d" % a, align_bytes=64) for a in range(PASSES)]
+        tok_plane = keep.tile([P, T], U8, name="tok_plane", align_bytes=64)
+        slot_codes = [keep.tile([P, SLOTS], U32, name="slot_codes%d" % a, align_bytes=64) for a in range(PASSES)]
+        slot_plane = keep.tile([P, SLOTS], U8, name="slot_plane", align_bytes=64)
+        relu = keep.tile([P, SLOTS + PAD], F32, name="relu")
+        y = keep.tile([P, SLOTS + PAD], F32, name="y")
+
+        nc.gpsimd.memset(tok_plane[:], 0)
+        nc.vector.memset(relu[:, SLOTS:], 0.0)
+        nc.vector.memset(w_plane[:].rearrange("p m n -> p (m n)").bitcast(I32), 0)
+        nc.scalar.activation(out=y[:, SLOTS:], in_=relu[:, SLOTS:], func=ACT.Square)
+
+        raw = {}
+        for a in range(PASSES):
+            rows = xT[a * P * PACK : (a + 1) * P * PACK, :].rearrange("(p j) t -> p j t", j=PACK)
+            t0 = 0
+            for c, (width, engine) in enumerate(CHUNKS[a]):
+                raw[a, c] = keep.tile([P, PACK, width], F32, name="raw%d_%d" % (a, c))
+                nc.sync.dma_start(out=raw[a, c][:], in_=rows[:, :, t0 : t0 + width])
+                t0 += width
+            if a == 0:
+                nc.sync.dma_start(offs_sb[:], offs)
+        scale_rows = w_scales.rearrange("e a q n -> q (e a) n").bitcast(I32)
+        for quad in range(4):
+            nc.sync.dma_start(out=w_plane[32 * quad : 32 * quad + 4, :, :].bitcast(I32), in_=scale_rows[4 * quad : 4 * quad + 4, :, :])
+        nc.sync.dma_start(out=bias[:], in_=b)
+        words = w_words.rearrange("e a p n r -> p (e a) (n r)").bitcast(I32)
+        for e0, e1 in W_LOADS:
+            nc.sync.dma_start(out=w_codes[:, e0 * PASSES : e1 * PASSES, :], in_=words[:, e0 * PASSES : e1 * PASSES, :])
+        for r, pos in enumerate((pos1, pos2, pos3)):
+            nc.sync.dma_start(pos_sb[r][:], pos)
+        for r in range(3):
+            nc.sync.dma_start(out=gates[r][:], in_=gate[r])
+
+        for a in range(PASSES):
+            t0 = 0
+            for c, (width, engine) in enumerate(CHUNKS[a]):
+                grouped = keep.tile([P, width, PACK], BF16, name="grouped%d_%d" % (a, c), align_bytes=64)
+                dst = grouped[:].rearrange("p (c i) j -> p c j i", i=4)
+                src = raw[a, c][:].rearrange("p j (c i) -> p c j i", i=4)
+                if engine == "v":
+                    nc.vector.tensor_copy(out=dst, in_=src)
+                else:
+                    nc.scalar.activation(out=dst, in_=src, func=ACT.Copy)
+                nc.vector.quantize_mx(
+                    out=tok_codes[a][:, t0 : t0 + width].bitcast(FP8X4),
+                    scales=tok_plane[4 * a : P, t0 : t0 + width],
+                    in_=grouped[:].rearrange("p t j -> p (t j)"),
+                )
+                t0 += width
+
+        def gather(dst, window, e0, e1):
+            entries = offs_sb[:, e0 * C // LANES : e1 * C // LANES]
+            nc.vector.tensor_copy(out=dst[:, e0 * C : e1 * C], in_=window[:].indirect(entries))
+
+        for a in range(2):
+            for e0, e1 in BYTE_PIECES:
+                gather(slot_codes[a], tok_codes[a], e0, e1)
+
+        for g, (e0, e1) in enumerate(BYTE_PIECES):
+            gather(slot_plane, tok_plane, e0, e1)
+            gather(slot_codes[2], tok_codes[2], e0, e1)
+            for f0, f1 in WORD_PIECES[g]:
+                gather(slot_codes[3], tok_codes[3], f0, f1)
+                for e in range(f0, f1):
+                    cols = slice(e * C, (e + 1) * C)
+                    acc = psum.tile([P, C], F32, name="acc")
+                    for a in range(PASSES):
+                        nc.tensor.matmul_mx(
+                            out=acc[:],
+                            lhsT=w_codes[:, e * PASSES + a, :].bitcast(FP8X4),
+                            lhsT_scale=w_plane[:, e * PASSES + a, :],
+                            rhs=slot_codes[a][:, cols].bitcast(FP8X4),
+                            rhs_scale=slot_plane[4 * a : P, cols],
+                            start=(a == 0),
+                            stop=(a == PASSES - 1),
+                        )
+                    nc.scalar.activation(out=relu[:, cols], in_=acc[:], func=ACT.Relu, bias=bias[:, e : e + 1])
+                nc.scalar.activation(out=y[:, f0 * C : f1 * C], in_=relu[:, f0 * C : f1 * C], func=ACT.Square)
+
+        terms = [keep.tile([P, T], F32, name="term%d" % r) for r in range(3)]
+        pair = keep.tile([P, T], F32, name="pair")
+        total = keep.tile([P, T], F32, name="total")
+
+        def weigh(r, t0, t1):
+            nc.vector.tensor_tensor(terms[r][:, t0:t1], y[:].indirect(pos_sb[r][:, t0 // LANES : t1 // LANES]), gates[r][:, t0:t1], ALU.mult)
+
+        def finish(t0, t1):
+            nc.vector.tensor_tensor(total[:, t0:t1], pair[:, t0:t1], terms[2][:, t0:t1], ALU.add)
+            nc.sync.dma_start(out=out[:, t0:t1], in_=total[:, t0:t1])
+
+        for i, (t0, t1) in enumerate(OUT_CHUNKS):
+            weigh(0, t0, t1)
+            if i > 0:
+                finish(*OUT_CHUNKS[i - 1])
+            weigh(1, t0, t1)
+            weigh(2, t0, t1)
+            nc.vector.tensor_tensor(pair[:, t0:t1], terms[0][:, t0:t1], terms[1][:, t0:t1], ALU.add)
+        finish(*OUT_CHUNKS[-1])

@@ -22,16 +22,16 @@ PACK = 4
 PASSES = K // (P * PACK)
 LANES = 16
 
-CHUNKS = [
-    [(256, "v"), (256, "v"), (128, "s"), (128, "v")],
-    [(256, "s"), (256, "s"), (256, "s")],
-    [(256, "s"), (256, "s"), (256, "s")],
-    [(256, "s"), (256, "s"), (256, "s")],
+LOADS = [
+    [[(256, "s")], [(256, "v")], [(128, "s"), (128, "v")]],
+    [[(256, "s")], [(256, "s")], [(256, "s")]],
+    [[(256, "s")], [(512, "s")]],
+    [[(512, "s")], [(256, "s")]],
 ]
 BYTE_PIECES = [(0, 4), (4, 8), (8, 12)]
 WORD_PIECES = [[(0, 4)], [(4, 8)], [(8, 11), (11, 12)]]
-W_LOADS = [(0, 4), (4, 8), (8, 12)]
-OUT_CHUNKS = [(0, 512), (512, 768)]
+W_LOADS = [(0, 4), (4, 8), (8, 11), (11, 12)]
+OUT_CHUNKS = [(0, 384), (384, 640), (640, 768)]
 
 
 def tile_moe_ecr_lin_relu2_kernel(tc, xT, w_words, w_scales, b, gate, offs, pos1, pos2, pos3, out):
@@ -53,49 +53,54 @@ def tile_moe_ecr_lin_relu2_kernel(tc, xT, w_words, w_scales, b, gate, offs, pos1
         relu = keep.tile([P, SLOTS + PAD], F32, name="relu")
         y = keep.tile([P, SLOTS + PAD], F32, name="y")
 
-        nc.gpsimd.memset(tok_plane[:], 0)
         nc.vector.memset(relu[:, SLOTS:], 0.0)
         nc.vector.memset(w_plane[:].rearrange("p m n -> p (m n)").bitcast(I32), 0)
+        nc.vector.memset(tok_plane[:].bitcast(I32), 0)
         nc.scalar.activation(out=y[:, SLOTS:], in_=relu[:, SLOTS:], func=ACT.Square)
 
+        scale_rows = w_scales.rearrange("e a q n -> q (e a) n").bitcast(I32)
+        for j in range(4):
+            nc.gpsimd.dma_start(out=w_plane[j:P:32, :, :].bitcast(I32), in_=scale_rows[j:16:4, :, :])
         raw = {}
         for a in range(PASSES):
             rows = xT[a * P * PACK : (a + 1) * P * PACK, :].rearrange("(p j) t -> p j t", j=PACK)
             t0 = 0
-            for c, (width, engine) in enumerate(CHUNKS[a]):
+            for c, casts in enumerate(LOADS[a]):
+                width = sum(w for w, engine in casts)
                 raw[a, c] = keep.tile([P, PACK, width], F32, name="raw%d_%d" % (a, c))
                 nc.sync.dma_start(out=raw[a, c][:], in_=rows[:, :, t0 : t0 + width])
                 t0 += width
             if a == 0:
                 nc.sync.dma_start(offs_sb[:], offs)
-        scale_rows = w_scales.rearrange("e a q n -> q (e a) n").bitcast(I32)
-        for quad in range(4):
-            nc.sync.dma_start(out=w_plane[32 * quad : 32 * quad + 4, :, :].bitcast(I32), in_=scale_rows[4 * quad : 4 * quad + 4, :, :])
-        nc.sync.dma_start(out=bias[:], in_=b)
+            if a == 2:
+                nc.sync.dma_start(out=bias[:], in_=b)
+                for r, pos in enumerate((pos1, pos2, pos3)):
+                    nc.sync.dma_start(pos_sb[r][:], pos)
         words = w_words.rearrange("e a p n r -> p (e a) (n r)").bitcast(I32)
         for e0, e1 in W_LOADS:
             nc.sync.dma_start(out=w_codes[:, e0 * PASSES : e1 * PASSES, :], in_=words[:, e0 * PASSES : e1 * PASSES, :])
-        for r, pos in enumerate((pos1, pos2, pos3)):
-            nc.sync.dma_start(pos_sb[r][:], pos)
         for r in range(3):
             nc.sync.dma_start(out=gates[r][:], in_=gate[r])
 
         for a in range(PASSES):
             t0 = 0
-            for c, (width, engine) in enumerate(CHUNKS[a]):
-                grouped = keep.tile([P, width, PACK], BF16, name="grouped%d_%d" % (a, c), align_bytes=64)
-                dst = grouped[:].rearrange("p (c i) j -> p c j i", i=4)
-                src = raw[a, c][:].rearrange("p j (c i) -> p c j i", i=4)
-                if engine == "v":
-                    nc.vector.tensor_copy(out=dst, in_=src)
-                else:
-                    nc.scalar.activation(out=dst, in_=src, func=ACT.Copy)
-                nc.vector.quantize_mx(
-                    out=tok_codes[a][:, t0 : t0 + width].bitcast(FP8X4),
-                    scales=tok_plane[4 * a : P, t0 : t0 + width],
-                    in_=grouped[:].rearrange("p t j -> p (t j)"),
-                )
-                t0 += width
+            for c, casts in enumerate(LOADS[a]):
+                c0 = 0
+                for width, engine in casts:
+                    grouped = keep.tile([P, width, PACK], BF16, name="grouped%d_%d" % (a, t0), align_bytes=64)
+                    dst = grouped[:].rearrange("p (c i) j -> p c j i", i=4)
+                    src = raw[a, c][:, :, c0 : c0 + width].rearrange("p j (c i) -> p c j i", i=4)
+                    if engine == "v":
+                        nc.vector.tensor_copy(out=dst, in_=src)
+                    else:
+                        nc.scalar.activation(out=dst, in_=src, func=ACT.Copy)
+                    nc.vector.quantize_mx(
+                        out=tok_codes[a][:, t0 : t0 + width].bitcast(FP8X4),
+                        scales=tok_plane[4 * a : P, t0 : t0 + width],
+                        in_=grouped[:].rearrange("p t j -> p (t j)"),
+                    )
+                    t0 += width
+                    c0 += width
 
         def gather(dst, window, e0, e1):
             entries = offs_sb[:, e0 * C // LANES : e1 * C // LANES]

@@ -30,7 +30,7 @@ LOADS = [
 ]
 BYTE_PIECES = [(0, 4), (4, 8), (8, 12)]
 WORD_PIECES = [[(0, 4)], [(4, 8)], [(8, 11), (11, 12)]]
-W_LOADS = [(0, 4), (4, 8), (8, 11), (11, 12)]
+W_LOADS = [(e, e + 1) for e in range(E)]
 OUT_CHUNKS = [(0, 384), (384, 640), (640, 768)]
 
 
@@ -59,8 +59,6 @@ def tile_moe_ecr_lin_relu2_kernel(tc, xT, w_words, w_scales, b, gate, offs, pos1
         nc.scalar.activation(out=y[:, SLOTS:], in_=relu[:, SLOTS:], func=ACT.Square)
 
         scale_rows = w_scales.rearrange("e a q n -> q (e a) n").bitcast(I32)
-        for j in range(4):
-            nc.gpsimd.dma_start(out=w_plane[j:P:32, :, :].bitcast(I32), in_=scale_rows[j:16:4, :, :])
         raw = {}
         for a in range(PASSES):
             rows = xT[a * P * PACK : (a + 1) * P * PACK, :].rearrange("(p j) t -> p j t", j=PACK)
@@ -76,6 +74,8 @@ def tile_moe_ecr_lin_relu2_kernel(tc, xT, w_words, w_scales, b, gate, offs, pos1
                 nc.sync.dma_start(out=bias[:], in_=b)
                 for r, pos in enumerate((pos1, pos2, pos3)):
                     nc.sync.dma_start(pos_sb[r][:], pos)
+        for j in range(4):
+            nc.sync.dma_start(out=w_plane[j:P:32, :, :].bitcast(I32), in_=scale_rows[j:16:4, :, :])
         words = w_words.rearrange("e a p n r -> p (e a) (n r)").bitcast(I32)
         for e0, e1 in W_LOADS:
             nc.sync.dma_start(out=w_codes[:, e0 * PASSES : e1 * PASSES, :], in_=words[:, e0 * PASSES : e1 * PASSES, :])

@@ -28,9 +28,7 @@ LOADS = [
     [[(256, "s")], [(512, "s")]],
     [[(512, "s")], [(256, "s")]],
 ]
-BYTE_PIECES = [(0, 4), (4, 8), (8, 12)]
-WORD_PIECES = [[(0, 4)], [(4, 8)], [(8, 11), (11, 12)]]
-W_LOADS = [(e, e + 1) for e in range(E)]
+THIRDS = [(0, 4), (4, 8), (8, 12)]
 OUT_CHUNKS = [(0, 384), (384, 640), (640, 768)]
 
 
@@ -45,7 +43,7 @@ def tile_moe_ecr_lin_relu2_kernel(tc, xT, w_words, w_scales, b, gate, offs, pos1
         bias = keep.tile([P, E], F32, name="bias")
         w_codes = keep.tile([P, E * PASSES, N], I32, name="w_codes", align_bytes=64)
         w_plane = keep.tile([P, E * PASSES, N], U8, name="w_plane", align_bytes=64)
-        gates = [keep.tile([P, T], F32, name="gates%d" % r) for r in range(3)]
+        gates = keep.tile([P, 3, T], F32, name="gates")
         tok_codes = [keep.tile([P, T], U32, name="tok_codes%d" % a, align_bytes=64) for a in range(PASSES)]
         tok_plane = keep.tile([P, T], U8, name="tok_plane", align_bytes=64)
         slot_codes = [keep.tile([P, SLOTS], U32, name="slot_codes%d" % a, align_bytes=64) for a in range(PASSES)]
@@ -72,81 +70,123 @@ def tile_moe_ecr_lin_relu2_kernel(tc, xT, w_words, w_scales, b, gate, offs, pos1
                 nc.sync.dma_start(offs_sb[:], offs)
             if a == 2:
                 nc.sync.dma_start(out=bias[:], in_=b)
-                for r, pos in enumerate((pos1, pos2, pos3)):
-                    nc.sync.dma_start(pos_sb[r][:], pos)
         for j in range(4):
             nc.sync.dma_start(out=w_plane[j:P:32, :, :].bitcast(I32), in_=scale_rows[j:16:4, :, :])
         words = w_words.rearrange("e a p n r -> p (e a) (n r)").bitcast(I32)
-        for e0, e1 in W_LOADS:
-            nc.sync.dma_start(out=w_codes[:, e0 * PASSES : e1 * PASSES, :], in_=words[:, e0 * PASSES : e1 * PASSES, :])
-        for r in range(3):
-            nc.sync.dma_start(out=gates[r][:], in_=gate[r])
+        cuts = [e * PASSES for e in range(E)] + [E * PASSES - 1, E * PASSES]
+        for m0, m1 in zip(cuts[:-1], cuts[1:]):
+            nc.sync.dma_start(out=w_codes[:, m0:m1, :], in_=words[:, m0:m1, :])
+        for r, pos in enumerate((pos1, pos2, pos3)):
+            nc.sync.dma_start(pos_sb[r][:], pos)
+            nc.sync.dma_start(out=gates[:, r, :], in_=gate[r])
 
+        pieces = []
         for a in range(PASSES):
+            pieces.append([])
             t0 = 0
             for c, casts in enumerate(LOADS[a]):
                 c0 = 0
                 for width, engine in casts:
                     grouped = keep.tile([P, width, PACK], BF16, name="grouped%d_%d" % (a, t0), align_bytes=64)
-                    dst = grouped[:].rearrange("p (c i) j -> p c j i", i=4)
-                    src = raw[a, c][:, :, c0 : c0 + width].rearrange("p j (c i) -> p c j i", i=4)
-                    if engine == "v":
-                        nc.vector.tensor_copy(out=dst, in_=src)
-                    else:
-                        nc.scalar.activation(out=dst, in_=src, func=ACT.Copy)
-                    nc.vector.quantize_mx(
-                        out=tok_codes[a][:, t0 : t0 + width].bitcast(FP8X4),
-                        scales=tok_plane[4 * a : P, t0 : t0 + width],
-                        in_=grouped[:].rearrange("p t j -> p (t j)"),
-                    )
+                    pieces[a].append((raw[a, c][:, :, c0 : c0 + width], grouped, t0, width, engine))
                     t0 += width
                     c0 += width
+
+        def cast(a, i):
+            rows, grouped, t0, width, engine = pieces[a][i]
+            dst = grouped[:].rearrange("p (c i) j -> p c j i", i=4)
+            src = rows.rearrange("p j (c i) -> p c j i", i=4)
+            if engine == "v":
+                nc.vector.tensor_copy(out=dst, in_=src)
+            else:
+                nc.scalar.activation(out=dst, in_=src, func=ACT.Copy)
+
+        def quantise(a, i):
+            rows, grouped, t0, width, engine = pieces[a][i]
+            nc.vector.quantize_mx(
+                out=tok_codes[a][:, t0 : t0 + width].bitcast(FP8X4),
+                scales=tok_plane[4 * a : P, t0 : t0 + width],
+                in_=grouped[:].rearrange("p t j -> p (t j)"),
+            )
 
         def gather(dst, window, e0, e1):
             entries = offs_sb[:, e0 * C // LANES : e1 * C // LANES]
             nc.vector.tensor_copy(out=dst[:, e0 * C : e1 * C], in_=window[:].indirect(entries))
 
-        for a in range(2):
-            for e0, e1 in BYTE_PIECES:
-                gather(slot_codes[a], tok_codes[a], e0, e1)
+        def words_of(a, e0, e1):
+            gather(slot_codes[a], tok_codes[a], e0, e1)
 
-        for g, (e0, e1) in enumerate(BYTE_PIECES):
-            gather(slot_plane, tok_plane, e0, e1)
-            gather(slot_codes[2], tok_codes[2], e0, e1)
-            for f0, f1 in WORD_PIECES[g]:
-                gather(slot_codes[3], tok_codes[3], f0, f1)
-                for e in range(f0, f1):
-                    cols = slice(e * C, (e + 1) * C)
-                    acc = psum.tile([P, C], F32, name="acc")
-                    for a in range(PASSES):
-                        nc.tensor.matmul_mx(
-                            out=acc[:],
-                            lhsT=w_codes[:, e * PASSES + a, :].bitcast(FP8X4),
-                            lhsT_scale=w_plane[:, e * PASSES + a, :],
-                            rhs=slot_codes[a][:, cols].bitcast(FP8X4),
-                            rhs_scale=slot_plane[4 * a : P, cols],
-                            start=(a == 0),
-                            stop=(a == PASSES - 1),
-                        )
+        def experts(e0, e1):
+            for e in range(e0, e1):
+                cols = slice(e * C, (e + 1) * C)
+                acc = psum.tile([P, C], F32, name="acc")
+                for a in range(PASSES):
+                    nc.tensor.matmul_mx(
+                        out=acc[:],
+                        lhsT=w_codes[:, e * PASSES + a, :].bitcast(FP8X4),
+                        lhsT_scale=w_plane[:, e * PASSES + a, :],
+                        rhs=slot_codes[a][:, cols].bitcast(FP8X4),
+                        rhs_scale=slot_plane[4 * a : P, cols],
+                        start=(a == 0),
+                        stop=(a == PASSES - 1),
+                    )
+                if e < E - 1:
                     nc.scalar.activation(out=relu[:, cols], in_=acc[:], func=ACT.Relu, bias=bias[:, e : e + 1])
-                nc.scalar.activation(out=y[:, f0 * C : f1 * C], in_=relu[:, f0 * C : f1 * C], func=ACT.Square)
+                else:
+                    nc.vector.tensor_scalar(relu[:, cols], acc[:], bias[:, e : e + 1], 0.0, ALU.add, ALU.max)
+            if e1 < E:
+                cols = slice(e0 * C, e1 * C)
+                nc.scalar.activation(out=y[:, cols], in_=relu[:, cols], func=ACT.Square)
+
+        for i in range(4):
+            cast(0, i)
+        for i in range(4):
+            quantise(0, i)
+        for a in range(1, PASSES):
+            for i in range(len(pieces[a])):
+                cast(a, i)
+
+        words_of(0, *THIRDS[0])
+        words_of(0, *THIRDS[1])
+        quantise(1, 0)
+        words_of(0, *THIRDS[2])
+        quantise(1, 1)
+        quantise(1, 2)
+        for a in (1, 2):
+            words_of(a, *THIRDS[0])
+            words_of(a, *THIRDS[1])
+            for i in range(len(pieces[a + 1])):
+                quantise(a + 1, i)
+            words_of(a, *THIRDS[2])
+
+        gather(slot_plane, tok_plane, 0, 2)
+        for e0 in range(0, E - 2, 2):
+            gather(slot_plane, tok_plane, e0 + 2, e0 + 4)
+            words_of(PASSES - 1, e0, e0 + 2)
+            experts(e0, e0 + 2)
+        words_of(PASSES - 1, E - 2, E - 1)
+        words_of(PASSES - 1, E - 1, E)
+        experts(E - 2, E - 1)
+        experts(E - 1, E)
+        last = slice((E - 1) * C, E * C)
+        nc.vector.tensor_tensor(y[:, last], relu[:, last], relu[:, last], ALU.mult)
 
         terms = [keep.tile([P, T], F32, name="term%d" % r) for r in range(3)]
         pair = keep.tile([P, T], F32, name="pair")
         total = keep.tile([P, T], F32, name="total")
 
         def weigh(r, t0, t1):
-            nc.vector.tensor_tensor(terms[r][:, t0:t1], y[:].indirect(pos_sb[r][:, t0 // LANES : t1 // LANES]), gates[r][:, t0:t1], ALU.mult)
+            nc.vector.tensor_tensor(terms[r][:, t0:t1], y[:].indirect(pos_sb[r][:, t0 // LANES : t1 // LANES]), gates[:, r, t0:t1], ALU.mult)
 
         def finish(t0, t1):
             nc.vector.tensor_tensor(total[:, t0:t1], pair[:, t0:t1], terms[2][:, t0:t1], ALU.add)
             nc.sync.dma_start(out=out[:, t0:t1], in_=total[:, t0:t1])
 
-        for i, (t0, t1) in enumerate(OUT_CHUNKS):
-            weigh(0, t0, t1)
-            if i > 0:
-                finish(*OUT_CHUNKS[i - 1])
-            weigh(1, t0, t1)
-            weigh(2, t0, t1)
-            nc.vector.tensor_tensor(pair[:, t0:t1], terms[0][:, t0:t1], terms[1][:, t0:t1], ALU.add)
+        weigh(0, 0, T)
+        weigh(1, 0, T)
+        weigh(2, *OUT_CHUNKS[0])
+        nc.vector.tensor_tensor(pair[:], terms[0][:], terms[1][:], ALU.add)
+        for i in range(1, len(OUT_CHUNKS)):
+            weigh(2, *OUT_CHUNKS[i])
+            finish(*OUT_CHUNKS[i - 1])
         finish(*OUT_CHUNKS[-1])

from contextlib import ExitStack

import concourse.mybir as mybir

K, T, E, C, N = 2048, 768, 12, 128, 128
PAD = 64
SLOTS = E * C
FLOPS = 2 * SLOTS * K * N

F32 = mybir.dt.float32
BF16 = mybir.dt.bfloat16
I32 = mybir.dt.int32
U32 = mybir.dt.uint32
U16 = mybir.dt.uint16
U8 = mybir.dt.uint8
FP8X4 = mybir.dt.float8_e4m3fn_x4
ACT = mybir.ActivationFunctionType
ALU = mybir.AluOpType

P = 128
PACK = 4
PASSES = K // (P * PACK)
LANES = 16

LOADS = [
    [[(256, "s")], [(256, "v")], [(128, "s"), (128, "v")]],
    [[(256, "s")], [(256, "s")], [(256, "s")]],
    [[(256, "s")], [(512, "s")]],
    [[(512, "s")], [(256, "s")]],
]
THIRDS = [(0, 4), (4, 8), (8, 12)]
OUT_CHUNKS = [(0, 384), (384, 640), (640, 768)]


def tile_moe_ecr_lin_relu2_kernel(tc, xT, w_words, w_scales, b, gate, offs, pos1, pos2, pos3, out):
    nc = tc.nc
    with ExitStack() as ctx:
        keep = ctx.enter_context(tc.tile_pool(name="keep", bufs=1))
        psum = ctx.enter_context(tc.psum_pool(name="psum", bufs=8))

        offs_sb = keep.tile([P, SLOTS // LANES], U16, name="offs_sb")
        pos_sb = [keep.tile([P, T // LANES], U16, name="pos_sb%d" % r) for r in range(3)]
        bias = keep.tile([P, E], F32, name="bias")
        w_codes = keep.tile([P, E * PASSES, N], I32, name="w_codes", align_bytes=64)
        w_plane = keep.tile([P, E * PASSES, N], U8, name="w_plane", align_bytes=64)
        gates = keep.tile([P, 3, T], F32, name="gates")
        tok_codes = [keep.tile([P, T], U32, name="tok_codes%d" % a, align_bytes=64) for a in range(PASSES)]
        tok_plane = keep.tile([P, T], U8, name="tok_plane", align_bytes=64)
        slot_codes = [keep.tile([P, SLOTS], U32, name="slot_codes%d" % a, align_bytes=64) for a in range(PASSES)]
        slot_plane = keep.tile([P, SLOTS], U8, name="slot_plane", align_bytes=64)
        relu = keep.tile([P, SLOTS + PAD], F32, name="relu")
        y = keep.tile([P, SLOTS + PAD], F32, name="y")

        nc.vector.memset(relu[:, SLOTS:], 0.0)
        nc.vector.memset(w_plane[:].rearrange("p m n -> p (m n)").bitcast(I32), 0)
        nc.vector.memset(tok_plane[:].bitcast(I32), 0)
        nc.scalar.activation(out=y[:, SLOTS:], in_=relu[:, SLOTS:], func=ACT.Square)

        scale_rows = w_scales.rearrange("e a q n -> q (e a) n").bitcast(I32)
        raw = {}
        for a in range(PASSES):
            rows = xT[a * P * PACK : (a + 1) * P * PACK, :].rearrange("(p j) t -> p j t", j=PACK)
            t0 = 0
            for c, casts in enumerate(LOADS[a]):
                width = sum(w for w, engine in casts)
                raw[a, c] = keep.tile([P, PACK, width], F32, name="raw%d_%d" % (a, c))
                nc.sync.dma_start(out=raw[a, c][:], in_=rows[:, :, t0 : t0 + width])
                t0 += width
            if a == 0:
                nc.sync.dma_start(offs_sb[:], offs)
            if a == 2:
                nc.sync.dma_start(out=bias[:], in_=b)
        for j in range(4):
            nc.sync.dma_start(out=w_plane[j:P:32, :, :].bitcast(I32), in_=scale_rows[j:16:4, :, :])
        words = w_words.rearrange("e a p n r -> p (e a) (n r)").bitcast(I32)
        cuts = [e * PASSES for e in range(E)] + [E * PASSES - 1, E * PASSES]
        for m0, m1 in zip(cuts[:-1], cuts[1:]):
            nc.sync.dma_start(out=w_codes[:, m0:m1, :], in_=words[:, m0:m1, :])
        for r, pos in enumerate((pos1, pos2, pos3)):
            nc.sync.dma_start(pos_sb[r][:], pos)
            nc.sync.dma_start(out=gates[:, r, :], in_=gate[r])

        pieces = []
        for a in range(PASSES):
            pieces.append([])
            t0 = 0
            for c, casts in enumerate(LOADS[a]):
                c0 = 0
                for width, engine in casts:
                    grouped = keep.tile([P, width, PACK], BF16, name="grouped%d_%d" % (a, t0), align_bytes=64)
                    pieces[a].append((raw[a, c][:, :, c0 : c0 + width], grouped, t0, width, engine))
                    t0 += width
                    c0 += width

        def cast(a, i):
            rows, grouped, t0, width, engine = pieces[a][i]
            dst = grouped[:].rearrange("p (c i) j -> p c j i", i=4)
            src = rows.rearrange("p j (c i) -> p c j i", i=4)
            if engine == "v":
                nc.vector.tensor_copy(out=dst, in_=src)
            else:
                nc.scalar.activation(out=dst, in_=src, func=ACT.Copy)

        def quantise(a, i):
            rows, grouped, t0, width, engine = pieces[a][i]
            nc.vector.quantize_mx(
                out=tok_codes[a][:, t0 : t0 + width].bitcast(FP8X4),
                scales=tok_plane[4 * a : P, t0 : t0 + width],
                in_=grouped[:].rearrange("p t j -> p (t j)"),
            )

        def gather(dst, window, e0, e1):
            entries = offs_sb[:, e0 * C // LANES : e1 * C // LANES]
            nc.vector.tensor_copy(out=dst[:, e0 * C : e1 * C], in_=window[:].indirect(entries))

        def words_of(a, e0, e1):
            gather(slot_codes[a], tok_codes[a], e0, e1)

        def experts(e0, e1):
            for e in range(e0, e1):
                cols = slice(e * C, (e + 1) * C)
                acc = psum.tile([P, C], F32, name="acc")
                for a in range(PASSES):
                    nc.tensor.matmul_mx(
                        out=acc[:],
                        lhsT=w_codes[:, e * PASSES + a, :].bitcast(FP8X4),
                        lhsT_scale=w_plane[:, e * PASSES + a, :],
                        rhs=slot_codes[a][:, cols].bitcast(FP8X4),
                        rhs_scale=slot_plane[4 * a : P, cols],
                        start=(a == 0),
                        stop=(a == PASSES - 1),
                    )
                if e < E - 1:
                    nc.scalar.activation(out=relu[:, cols], in_=acc[:], func=ACT.Relu, bias=bias[:, e : e + 1])
                else:
                    nc.vector.tensor_scalar(relu[:, cols], acc[:], bias[:, e : e + 1], 0.0, ALU.add, ALU.max)
            if e1 < E:
                cols = slice(e0 * C, e1 * C)
                nc.scalar.activation(out=y[:, cols], in_=relu[:, cols], func=ACT.Square)

        for i in range(4):
            cast(0, i)
        for i in range(4):
            quantise(0, i)
        for a in range(1, PASSES):
            for i in range(len(pieces[a])):
                cast(a, i)

        words_of(0, *THIRDS[0])
        words_of(0, *THIRDS[1])
        quantise(1, 0)
        words_of(0, *THIRDS[2])
        quantise(1, 1)
        quantise(1, 2)
        for a in (1, 2):
            words_of(a, *THIRDS[0])
            words_of(a, *THIRDS[1])
            for i in range(len(pieces[a + 1])):
                quantise(a + 1, i)
            words_of(a, *THIRDS[2])

        gather(slot_plane, tok_plane, 0, 2)
        for e0 in range(0, E - 2, 2):
            gather(slot_plane, tok_plane, e0 + 2, e0 + 4)
            words_of(PASSES - 1, e0, e0 + 2)
            experts(e0, e0 + 2)
        words_of(PASSES - 1, E - 2, E - 1)
        words_of(PASSES - 1, E - 1, E)
        experts(E - 2, E - 1)
        experts(E - 1, E)
        last = slice((E - 1) * C, E * C)
        nc.vector.tensor_tensor(y[:, last], relu[:, last], relu[:, last], ALU.mult)

        terms = [keep.tile([P, T], F32, name="term%d" % r) for r in range(3)]
        pair = keep.tile([P, T], F32, name="pair")
        total = keep.tile([P, T], F32, name="total")

        def weigh(r, t0, t1):
            nc.vector.tensor_tensor(terms[r][:, t0:t1], y[:].indirect(pos_sb[r][:, t0 // LANES : t1 // LANES]), gates[:, r, t0:t1], ALU.mult)

        def finish(t0, t1):
            nc.vector.tensor_tensor(total[:, t0:t1], pair[:, t0:t1], terms[2][:, t0:t1], ALU.add)
            nc.sync.dma_start(out=out[:, t0:t1], in_=total[:, t0:t1])

        weigh(0, 0, T)
        weigh(1, 0, T)
        weigh(2, *OUT_CHUNKS[0])
        nc.vector.tensor_tensor(pair[:], terms[0][:], terms[1][:], ALU.add)
        for i in range(1, len(OUT_CHUNKS)):
            weigh(2, *OUT_CHUNKS[i])
            finish(*OUT_CHUNKS[i - 1])
        finish(*OUT_CHUNKS[-1])
